import numpy as np
import ml_dtypes


def mxq(x, axis, fmt="e4m3"):
    dtype, down = {"e4m3": (ml_dtypes.float8_e4m3fn, 7), "e5m2": (ml_dtypes.float8_e5m2, 14)}[fmt]
    v = np.moveaxis(np.asarray(x, np.float32).astype(ml_dtypes.bfloat16).astype(np.float64), axis, -1)
    blocks = v.reshape(v.shape[:-1] + (-1, 32))
    amax = np.abs(blocks).max(-1, keepdims=True)
    byte = np.maximum(np.where(amax > 0, np.frexp(amax)[1] - 1 + 127, 0) - down, 1)
    scale = np.exp2(byte - 127.0)
    codes = (blocks / scale).astype(np.float32).astype(dtype).astype(np.float64)
    return np.moveaxis((codes * scale).reshape(v.shape), -1, axis)


WIDE = False


def mx_kscale(k):
    if not WIDE:
        return np.ones(k)
    levels = np.array([10, -10, 5, -5, 0])
    if k % 512:
        return np.exp2(np.random.permutation(np.resize(levels, k // 32))).repeat(32)
    a = np.empty((k // 512, 16))
    for p in range(k // 512):
        a[p, :8] = np.random.permutation(np.resize(levels, 8))
        for g in range(8):
            far = levels[np.abs(levels - a[p, g]) >= 10]
            a[p, g + 8] = far[np.random.randint(len(far))]
    return np.exp2(a.ravel()).repeat(32)


def f64(x):
    return np.asarray(x).astype(np.float64)


def striped(idx):
    return np.tile(idx.reshape(-1, 16).T, (8, 1)).astype(np.uint16)


def unstriped(offs):
    return offs[:16].T.reshape(-1).astype(np.int64)


def striped8(idx):
    return np.concatenate([x.reshape(-1, 16).T for x in idx]).astype(np.uint16)


def runs(offs, k):
    lists = np.stack([offs[16 * r : 16 * r + 16].T.reshape(-1) for r in range(8)]).astype(np.int64)
    return lists[np.arange(k) % 512 // 64]


def pack_weight(w):
    k, n = w.shape
    w = f64(np.asarray(w, np.float32).astype(ml_dtypes.bfloat16)).reshape(k // 32, 32, n)
    amax = np.abs(w).max(1)
    byte = np.clip(np.where(amax > 0, np.frexp(amax)[1] - 1 + 127 - 7, 1), 1, 254)
    scaled = (w * np.exp2(127.0 - byte)[:, None, :]).reshape(k, n).astype(np.float32)
    words = np.ascontiguousarray(scaled.reshape(k // 512, 128, 4, n).transpose(0, 1, 3, 2)).astype(ml_dtypes.float8_e4m3fn).view(np.uint8)
    return words, np.ascontiguousarray(byte.astype(np.uint8).reshape(k // 512, 16, n))


def unpack_weight(words, scales):
    g, p, n, _ = words.shape
    vals = np.ascontiguousarray(words).view(ml_dtypes.float8_e4m3fn).astype(np.float64) * np.repeat(np.exp2(scales.astype(np.float64) - 127.0), 8, axis=1)[..., None]
    return vals.transpose(0, 1, 3, 2).reshape(g * 512, n)


def relu(v):
    return np.maximum(v, 0.0)


def sigmoid(v):
    return 1.0 / (1.0 + np.exp(-np.maximum(v, -700.0)))


K, T, S, N, H = 512, 2048, 512, 512, 512


def setup_inputs():
    n = np.random.standard_normal
    s = mx_kscale(K)[:, None]
    u = mx_kscale(H)
    packed_xT = pack_weight(n((K, T)) * s)
    return {
        "x_words": packed_xT[0],
        "x_scales": packed_xT[1],
        "w1": (n((K, H)) / np.sqrt(K) / s).astype(np.float32),
        "gn": (np.random.uniform(0.5, 1.5, (H, 1)) * u[:, None]).astype(np.float32),
        "w2": (n((H, N)) / np.sqrt(H) / u[:, None]).astype(np.float32),
        "offs": striped(np.random.permutation(T)[:S]),
        "c1": striped8(np.stack([np.random.permutation(S) for _ in range(8)])),
        "c2": striped8(np.stack([np.random.permutation(S) for _ in range(8)])),
        "c3": striped8(np.stack([np.random.permutation(S) for _ in range(8)])),
    }


def reference(x_words, x_scales, w1, gn, w2, offs, c1, c2, c3):
    xq = unpack_weight(x_words, x_scales)[:, unstriped(offs)]
    p = sigmoid(2.0 * ((mxq(f64(w1), 0, "e4m3").T @ xq)))
    a = p[np.arange(H)[:, None], runs(c1, H)]
    c = p[np.arange(H)[:, None], runs(c3, H)]
    b = p[np.arange(H)[:, None], runs(c2, H)]
    z = f64(gn) * (np.maximum(relu(a + c + -1), np.clip(b - a + 1, 0.0, 1.0) + -0.5))
    return mxq(f64(w2), 0, "e4m3").T @ mxq(z, 0, "e4m3")

@@ -1,0 +1,170 @@
+from contextlib import ExitStack
+
+import concourse.mybir as mybir
+
+K, T, S, N, H = 512, 2048, 512, 512, 512
+FLOPS = 2 * K * H * S + 2 * H * N * S
+
+F32 = mybir.dt.float32
+BF16 = mybir.dt.bfloat16
+I32 = mybir.dt.int32
+U32 = mybir.dt.uint32
+U16 = mybir.dt.uint16
+U8 = mybir.dt.uint8
+FP8X4 = mybir.dt.float8_e4m3fn_x4
+ALU = mybir.AluOpType
+ACT = mybir.ActivationFunctionType
+
+P = 128
+PACK = 4
+CHUNKS = (256, 128, 128)
+PIECE = 256
+W1_SCALAR_M = 64
+
+
+def tile_picked_lukaslog_none_p_kernel(tc, x_words, x_scales, w1, gn, w2, offs, c1, c2, c3, out):
+    nc = tc.nc
+    with ExitStack() as ctx:
+        keep = ctx.enter_context(tc.tile_pool(name="keep", bufs=1))
+        psum = ctx.enter_context(tc.psum_pool(name="psum", bufs=1))
+
+        x_scale_table = keep.tile([P, T], U8, align_bytes=64, tag="late")
+        nc.vector.memset(x_scale_table[:].bitcast(I32), 0)
+
+        offs_sb = keep.tile([P, S // 16], U16)
+        nc.sync.dma_start(offs_sb[:], offs)
+        c1_sb = keep.tile([P, S // 16], U16)
+        nc.sync.dma_start(c1_sb[:], c1)
+        w1_raw = keep.tile([P, PACK, H], F32)
+        nc.sync.dma_start(w1_raw[:], w1.rearrange("(p j) h -> p j h", j=PACK))
+        for q in range(4):
+            nc.scalar.dma_start(
+                x_scale_table[32 * q : 32 * q + 4, :].bitcast(I32),
+                x_scales[0, 4 * q : 4 * q + 4, :].bitcast(I32),
+            )
+        x_word_table = keep.tile([P, T], I32, align_bytes=64)
+        nc.sync.dma_start(x_word_table[:], x_words[0].rearrange("p n j -> p (n j)").bitcast(I32))
+        c3_sb = keep.tile([P, S // 16], U16)
+        nc.sync.dma_start(c3_sb[:], c3)
+        c2_sb = keep.tile([P, S // 16], U16)
+        nc.sync.dma_start(c2_sb[:], c2)
+        gain = keep.tile([P, PACK], F32)
+        nc.gpsimd.dma_start(gain[:], gn.rearrange("(p t) o -> p (t o)", t=PACK))
+
+        x_scale = keep.tile([P, S], U8, align_bytes=64)
+        nc.vector.tensor_copy(x_scale[:], x_scale_table[:].indirect(offs_sb[:]))
+        w2_raw = keep.tile([P, PACK, N], F32, align_bytes=64, tag="late")
+        nc.sync.dma_start(w2_raw[:], w2.rearrange("(p j) n -> p j n", j=PACK))
+
+        w1_bf = keep.tile([P, PACK, P, PACK], BF16, align_bytes=64)
+        w1_dst = w1_bf[:].rearrange("p t m j -> p m j t")
+        w1_src = w1_raw[:].rearrange("p j (m t) -> p m j t", t=PACK)
+        nc.scalar.copy(w1_dst[:, :W1_SCALAR_M], w1_src[:, :W1_SCALAR_M])
+        nc.vector.tensor_copy(w1_dst[:, W1_SCALAR_M:], w1_src[:, W1_SCALAR_M:])
+        w1_code = keep.tile([P, H], U32, align_bytes=64)
+        w1_scale = keep.tile([P, H], U8, align_bytes=64)
+        nc.vector.quantize_mx(w1_code[:].bitcast(FP8X4), w1_scale[:], w1_bf[:].rearrange("p t m j -> p (t m j)"))
+
+        x_code = keep.tile([P, S], U32, align_bytes=64)
+        truth = keep.tile([P, S], F32)
+        logit = [keep.tile([P, S], F32, name=f"logit{t}") for t in range(3)]
+
+        def first_product(t, j0, width, bank):
+            cols = slice(t * P, (t + 1) * P)
+            hid = psum.tile([P, width], F32, tag=f"bank{bank}")
+            nc.tensor.matmul_mx(hid[:], w1_code[:, cols].bitcast(FP8X4), w1_scale[:, cols],
+                                x_code[:, j0 : j0 + width].bitcast(FP8X4), x_scale[:, j0 : j0 + width], start=True, stop=True)
+            return hid
+
+        for h in range(2):
+            cols = slice(h * PIECE, (h + 1) * PIECE)
+            nc.vector.tensor_copy(x_code[:, cols], x_word_table[:].bitcast(U32).indirect(offs_sb[:, h * PIECE // 16 : (h + 1) * PIECE // 16]))
+            hid3 = first_product(3, h * PIECE, PIECE, h)
+            hid0 = first_product(0, h * PIECE, PIECE, 2 + h)
+            nc.scalar.activation(truth[:, cols], hid3[:], ACT.Sigmoid, scale=2.0)
+            if h == 0:
+                nc.scalar.copy(logit[0][:, cols], hid0[:])
+            else:
+                nc.vector.tensor_copy(logit[0][:, cols], hid0[:])
+        hid = {t: first_product(t, 0, S, 3 + t) for t in (1, 2)}
+
+        conj = keep.tile([P, PACK, S], F32)
+        impl = keep.tile([P, PACK, S], F32)
+        a_less = keep.tile([P, S], F32)
+        truth_less = keep.tile([P, S], F32)
+        for j0 in range(0, S, PIECE):
+            cols = slice(j0, j0 + PIECE)
+            lcols = slice(j0 // 16, (j0 + PIECE) // 16)
+            nc.vector.tensor_scalar(a_less[:, cols], truth[:].indirect(c1_sb[:, lcols]), 1.0, -1.0, ALU.mult, ALU.add)
+        nc.vector.tensor_scalar(truth_less[:], truth[:], -0.5, None, ALU.add)
+        for j0 in range(0, S, PIECE):
+            cols = slice(j0, j0 + PIECE)
+            lcols = slice(j0 // 16, (j0 + PIECE) // 16)
+            nc.vector.tensor_tensor(conj[:, 3, cols], truth[:].indirect(c3_sb[:, lcols]), a_less[:, cols], ALU.add)
+            nc.vector.tensor_tensor(impl[:, 3, cols], truth_less[:].indirect(c2_sb[:, lcols]), a_less[:, cols], ALU.subtract)
+
+        w2_bf = keep.tile([P, N, PACK], BF16, align_bytes=64)
+        nc.vector.tensor_copy(
+            w2_bf[:].rearrange("p (c i) j -> p c j i", i=4),
+            w2_raw[:].rearrange("p j (c i) -> p c j i", i=4),
+        )
+        w2_code = keep.tile([P, N], U32, align_bytes=64)
+        w2_scale = keep.tile([P, N], U8, align_bytes=64)
+        nc.vector.quantize_mx(w2_code[:].bitcast(FP8X4), w2_scale[:], w2_bf[:].rearrange("p n j -> p (n j)"))
+
+        a_val = keep.tile([P, 3, S], F32)
+        b_val = keep.tile([P, 3, S], F32)
+        c_val = keep.tile([P, 3, S], F32)
+        best = keep.tile([P, PACK, S], F32)
+        z_rows = keep.tile([P, PACK, S], BF16)
+        z_bf = keep.tile([P, S, PACK], BF16, align_bytes=64)
+        z_code = keep.tile([P, S], U32, align_bytes=64)
+        z_scale = keep.tile([P, S], U8, align_bytes=64)
+        out_view = out.rearrange("(u p) j -> p u j", p=P)
+
+        def look_up(j0, width):
+            cols = slice(j0, j0 + width)
+            lcols = slice(j0 // 16, (j0 + width) // 16)
+            for t in range(3):
+                if j0 == 0 and t > 0:
+                    nc.scalar.copy(logit[t][:], hid[t][:])
+                for val, lst in ((a_val, c1_sb), (c_val, c3_sb), (b_val, c2_sb)):
+                    nc.scalar.activation(val[:, t, cols], logit[t][:].indirect(lst[:, lcols]), ACT.Sigmoid, scale=2.0)
+
+        def logic(j0, width):
+            cols = slice(j0, j0 + width)
+            for t in range(3):
+                nc.vector.scalar_tensor_tensor(conj[:, t, cols], a_val[:, t, cols], -1.0, c_val[:, t, cols], ALU.add, ALU.add)
+                nc.vector.scalar_tensor_tensor(impl[:, t, cols], b_val[:, t, cols], 0.5, a_val[:, t, cols], ALU.add, ALU.subtract)
+            for t in (3, 0, 1, 2):
+                nc.vector.scalar_tensor_tensor(best[:, t, cols], impl[:, t, cols], 0.5, conj[:, t, cols], ALU.min, ALU.max)
+            for t in (3, 0, 1, 2):
+                nc.vector.tensor_scalar(z_rows[:, t, cols], best[:, t, cols], 0.0, gain[:, t : t + 1], ALU.max, ALU.mult)
+            nc.vector.tensor_copy(
+                z_bf[:, cols, :].rearrange("p (c i) t -> p c t i", i=4),
+                z_rows[:, :, cols].rearrange("p t (c i) -> p c t i", i=4),
+            )
+            nc.vector.quantize_mx(z_code[:, cols].bitcast(FP8X4), z_scale[:, cols], z_bf[:, cols, :].rearrange("p j t -> p (j t)"))
+
+        def project(j0, width, bank, last):
+            cols = slice(j0, j0 + width)
+            for half in range(2):
+                acc = psum.tile([P, 2, width], F32, tag=f"bank{bank + half}")
+                for u in range(2):
+                    m = slice((2 * half + u) * P, (2 * half + u + 1) * P)
+                    nc.tensor.matmul_mx(acc[:, u, :], w2_code[:, m].bitcast(FP8X4), w2_scale[:, m],
+                                        z_code[:, cols].bitcast(FP8X4), z_scale[:, cols], start=True, stop=True)
+                res = keep.tile([P, 2, width], F32, name=f"res{j0}_{half}")
+                if last and half == 1:
+                    nc.vector.tensor_copy(res[:], acc[:])
+                    nc.sync.dma_start(out_view[:, 2 * half : 2 * half + 2, cols], res[:])
+                else:
+                    nc.scalar.copy(res[:], acc[:])
+                    nc.sync.dma_start(out_view[:, 2 * half : 2 * half + 2, cols], res[:])
+
+        starts = [sum(CHUNKS[:i]) for i in range(len(CHUNKS))]
+        for i, (j0, width) in enumerate(zip(starts, CHUNKS)):
+            look_up(j0, width)
+            logic(j0, width)
+        for i, (j0, width) in enumerate(zip(starts, CHUNKS)):
+            project(j0, width, (6 + 2 * i) % 8, i == len(CHUNKS) - 1)

@@ -19,7 +19,7 @@ P = 128
 PACK = 4
 CHUNKS = (256, 128, 128)
 PIECE = 256
-W1_SCALAR_M = 64
+W1_SCALAR_M = 72
 
 
 def tile_picked_lukaslog_none_p_kernel(tc, x_words, x_scales, w1, gn, w2, offs, c1, c2, c3, out):
@@ -28,46 +28,53 @@ def tile_picked_lukaslog_none_p_kernel(tc, x_words, x_scales, w1, gn, w2, offs, 
         keep = ctx.enter_context(tc.tile_pool(name="keep", bufs=1))
         psum = ctx.enter_context(tc.psum_pool(name="psum", bufs=1))
 
-        x_scale_table = keep.tile([P, T], U8, align_bytes=64, tag="late")
+        x_scale_table = keep.tile([P, T], U8, align_bytes=64, tag="scale_table_then_w1_code")
         nc.vector.memset(x_scale_table[:].bitcast(I32), 0)
+
+        warm_in = keep.tile([P, 1], F32)
+        nc.gpsimd.memset(warm_in[:], 0.0)
+        warm_out = keep.tile([P, 1], F32)
+        nc.scalar.activation(warm_out[:], warm_in[:], ACT.Sigmoid, scale=2.0)
 
         offs_sb = keep.tile([P, S // 16], U16)
         nc.sync.dma_start(offs_sb[:], offs)
-        c1_sb = keep.tile([P, S // 16], U16)
-        nc.sync.dma_start(c1_sb[:], c1)
         w1_raw = keep.tile([P, PACK, H], F32)
         nc.sync.dma_start(w1_raw[:], w1.rearrange("(p j) h -> p j h", j=PACK))
         for q in range(4):
-            nc.scalar.dma_start(
+            nc.sync.dma_start(
                 x_scale_table[32 * q : 32 * q + 4, :].bitcast(I32),
                 x_scales[0, 4 * q : 4 * q + 4, :].bitcast(I32),
             )
         x_word_table = keep.tile([P, T], I32, align_bytes=64)
         nc.sync.dma_start(x_word_table[:], x_words[0].rearrange("p n j -> p (n j)").bitcast(I32))
+        c1_sb = keep.tile([P, S // 16], U16)
+        nc.sync.dma_start(c1_sb[:], c1)
         c3_sb = keep.tile([P, S // 16], U16)
         nc.sync.dma_start(c3_sb[:], c3)
         c2_sb = keep.tile([P, S // 16], U16)
         nc.sync.dma_start(c2_sb[:], c2)
-        gain = keep.tile([P, PACK], F32)
-        nc.gpsimd.dma_start(gain[:], gn.rearrange("(p t) o -> p (t o)", t=PACK))
-
-        x_scale = keep.tile([P, S], U8, align_bytes=64)
-        nc.vector.tensor_copy(x_scale[:], x_scale_table[:].indirect(offs_sb[:]))
-        w2_raw = keep.tile([P, PACK, N], F32, align_bytes=64, tag="late")
+        w2_raw = keep.tile([P, PACK, N], F32)
         nc.sync.dma_start(w2_raw[:], w2.rearrange("(p j) n -> p j n", j=PACK))
+        gain = keep.tile([P, PACK], F32)
+        nc.sync.dma_start(gain[:], gn.rearrange("(p t) o -> p (t o)", t=PACK))
 
         w1_bf = keep.tile([P, PACK, P, PACK], BF16, align_bytes=64)
         w1_dst = w1_bf[:].rearrange("p t m j -> p m j t")
         w1_src = w1_raw[:].rearrange("p j (m t) -> p m j t", t=PACK)
         nc.scalar.copy(w1_dst[:, :W1_SCALAR_M], w1_src[:, :W1_SCALAR_M])
         nc.vector.tensor_copy(w1_dst[:, W1_SCALAR_M:], w1_src[:, W1_SCALAR_M:])
-        w1_code = keep.tile([P, H], U32, align_bytes=64)
+        x_scale = keep.tile([P, S], U8, align_bytes=64)
+        nc.vector.tensor_copy(x_scale[:], x_scale_table[:].indirect(offs_sb[:]))
+        w1_code = keep.tile([P, H], U32, align_bytes=64, tag="scale_table_then_w1_code")
         w1_scale = keep.tile([P, H], U8, align_bytes=64)
-        nc.vector.quantize_mx(w1_code[:].bitcast(FP8X4), w1_scale[:], w1_bf[:].rearrange("p t m j -> p (t m j)"))
+
+        def quantize_w1(t0):
+            cols = slice(t0 * P, (t0 + 2) * P)
+            nc.vector.quantize_mx(w1_code[:, cols].bitcast(FP8X4), w1_scale[:, cols], w1_bf[:, t0 : t0 + 2].rearrange("p t m j -> p (t m j)"))
 
         x_code = keep.tile([P, S], U32, align_bytes=64)
         truth = keep.tile([P, S], F32)
-        logit = [keep.tile([P, S], F32, name=f"logit{t}") for t in range(3)]
+        logit = {t: keep.tile([P, S], F32, name=f"logit{t}") for t in (1, 2, 3)}
 
         def first_product(t, j0, width, bank):
             cols = slice(t * P, (t + 1) * P)
@@ -76,95 +83,120 @@ def tile_picked_lukaslog_none_p_kernel(tc, x_words, x_scales, w1, gn, w2, offs, 
                                 x_code[:, j0 : j0 + width].bitcast(FP8X4), x_scale[:, j0 : j0 + width], start=True, stop=True)
             return hid
 
+        quantize_w1(0)
         for h in range(2):
             cols = slice(h * PIECE, (h + 1) * PIECE)
             nc.vector.tensor_copy(x_code[:, cols], x_word_table[:].bitcast(U32).indirect(offs_sb[:, h * PIECE // 16 : (h + 1) * PIECE // 16]))
-            hid3 = first_product(3, h * PIECE, PIECE, h)
-            hid0 = first_product(0, h * PIECE, PIECE, 2 + h)
-            nc.scalar.activation(truth[:, cols], hid3[:], ACT.Sigmoid, scale=2.0)
-            if h == 0:
-                nc.scalar.copy(logit[0][:, cols], hid0[:])
-            else:
-                nc.vector.tensor_copy(logit[0][:, cols], hid0[:])
-        hid = {t: first_product(t, 0, S, 3 + t) for t in (1, 2)}
+            hid0 = first_product(0, h * PIECE, PIECE, h)
+            hid1 = first_product(1, h * PIECE, PIECE, 2 + h)
+            nc.scalar.activation(truth[:, cols], hid0[:], ACT.Sigmoid, scale=2.0)
+            nc.scalar.copy(logit[1][:, cols], hid1[:])
+        quantize_w1(2)
+        hid = {t: first_product(t, 0, S, 2 + t) for t in (2, 3)}
 
         conj = keep.tile([P, PACK, S], F32)
         impl = keep.tile([P, PACK, S], F32)
-        a_less = keep.tile([P, S], F32)
+        a_val = keep.tile([P, PACK, S], F32)
+        b_val = keep.tile([P, PACK, S], F32)
+        c_val = keep.tile([P, PACK, S], F32)
+        best = keep.tile([P, PACK, S], F32)
+        z_rows = keep.tile([P, PACK, S], BF16)
+        z_bf = keep.tile([P, S, PACK], BF16, align_bytes=64)
+        z_code = keep.tile([P, S], U32, align_bytes=64)
+        z_scale = keep.tile([P, S], U8, align_bytes=64)
         truth_less = keep.tile([P, S], F32)
-        for j0 in range(0, S, PIECE):
-            cols = slice(j0, j0 + PIECE)
-            lcols = slice(j0 // 16, (j0 + PIECE) // 16)
-            nc.vector.tensor_scalar(a_less[:, cols], truth[:].indirect(c1_sb[:, lcols]), 1.0, -1.0, ALU.mult, ALU.add)
-        nc.vector.tensor_scalar(truth_less[:], truth[:], -0.5, None, ALU.add)
-        for j0 in range(0, S, PIECE):
-            cols = slice(j0, j0 + PIECE)
-            lcols = slice(j0 // 16, (j0 + PIECE) // 16)
-            nc.vector.tensor_tensor(conj[:, 3, cols], truth[:].indirect(c3_sb[:, lcols]), a_less[:, cols], ALU.add)
-            nc.vector.tensor_tensor(impl[:, 3, cols], truth_less[:].indirect(c2_sb[:, lcols]), a_less[:, cols], ALU.subtract)
+        out_view = out.rearrange("(u p) j -> p u j", p=P)
+
+        def entries(lst, cols):
+            return lst[:, cols.start // 16 : cols.stop // 16]
+
+        def look_up(t, cols):
+            if cols.start == 0 and t > 1:
+                nc.scalar.copy(logit[t][:], hid[t][:])
+            for val, lst in ((a_val, c1_sb), (c_val, c3_sb), (b_val, c2_sb)):
+                nc.scalar.activation(val[:, t, cols], logit[t][:].indirect(entries(lst, cols)), ACT.Sigmoid, scale=2.0)
+
+        def conjunction(ts, cols):
+            nc.vector.scalar_tensor_tensor(conj[:, ts, cols], a_val[:, ts, cols], -1.0, c_val[:, ts, cols], ALU.add, ALU.add)
+
+        def implication(ts, cols):
+            nc.vector.scalar_tensor_tensor(impl[:, ts, cols], b_val[:, ts, cols], 0.5, a_val[:, ts, cols], ALU.add, ALU.subtract)
+
+        def larger(ts, cols):
+            nc.vector.scalar_tensor_tensor(best[:, ts, cols], impl[:, ts, cols], 0.5, conj[:, ts, cols], ALU.min, ALU.max)
+
+        def scale_rows(ts, cols):
+            for t in range(ts.start, ts.stop):
+                nc.vector.tensor_scalar(z_rows[:, t, cols], best[:, t, cols], 0.0, gain[:, t : t + 1], ALU.max, ALU.mult)
+
+        def interleave(cols):
+            nc.vector.tensor_copy(
+                z_bf[:, cols, :].rearrange("p (c i) t -> p c t i", i=4),
+                z_rows[:, :, cols].rearrange("p t (c i) -> p c t i", i=4),
+            )
+
+        def quantize_z(cols):
+            nc.vector.quantize_mx(z_code[:, cols].bitcast(FP8X4), z_scale[:, cols], z_bf[:, cols, :].rearrange("p j t -> p (j t)"))
+
+        nc.scalar.activation(truth_less[:], truth[:], ACT.Copy, bias=-0.5)
+        pieces = [slice(j0, j0 + PIECE) for j0 in range(0, S, PIECE)]
+        for cols in pieces:
+            nc.vector.tensor_scalar(a_val[:, 0, cols], truth[:].indirect(entries(c1_sb, cols)), 1.0, -1.0, ALU.mult, ALU.add)
+        for cols in pieces:
+            nc.vector.tensor_tensor(conj[:, 0, cols], truth[:].indirect(entries(c3_sb, cols)), a_val[:, 0, cols], ALU.add)
+            nc.vector.tensor_tensor(impl[:, 0, cols], truth_less[:].indirect(entries(c2_sb, cols)), a_val[:, 0, cols], ALU.subtract)
 
         w2_bf = keep.tile([P, N, PACK], BF16, align_bytes=64)
         nc.vector.tensor_copy(
             w2_bf[:].rearrange("p (c i) j -> p c j i", i=4),
             w2_raw[:].rearrange("p j (c i) -> p c j i", i=4),
         )
+        larger(slice(0, 1), slice(0, S))
         w2_code = keep.tile([P, N], U32, align_bytes=64)
         w2_scale = keep.tile([P, N], U8, align_bytes=64)
         nc.vector.quantize_mx(w2_code[:].bitcast(FP8X4), w2_scale[:], w2_bf[:].rearrange("p n j -> p (n j)"))
+        scale_rows(slice(0, 1), slice(0, S))
 
-        a_val = keep.tile([P, 3, S], F32)
-        b_val = keep.tile([P, 3, S], F32)
-        c_val = keep.tile([P, 3, S], F32)
-        best = keep.tile([P, PACK, S], F32)
-        z_rows = keep.tile([P, PACK, S], BF16)
-        z_bf = keep.tile([P, S, PACK], BF16, align_bytes=64)
-        z_code = keep.tile([P, S], U32, align_bytes=64)
-        z_scale = keep.tile([P, S], U8, align_bytes=64)
-        out_view = out.rearrange("(u p) j -> p u j", p=P)
-
-        def look_up(j0, width):
-            cols = slice(j0, j0 + width)
-            lcols = slice(j0 // 16, (j0 + width) // 16)
-            for t in range(3):
-                if j0 == 0 and t > 0:
-                    nc.scalar.copy(logit[t][:], hid[t][:])
-                for val, lst in ((a_val, c1_sb), (c_val, c3_sb), (b_val, c2_sb)):
-                    nc.scalar.activation(val[:, t, cols], logit[t][:].indirect(lst[:, lcols]), ACT.Sigmoid, scale=2.0)
-
-        def logic(j0, width):
-            cols = slice(j0, j0 + width)
-            for t in range(3):
-                nc.vector.scalar_tensor_tensor(conj[:, t, cols], a_val[:, t, cols], -1.0, c_val[:, t, cols], ALU.add, ALU.add)
-                nc.vector.scalar_tensor_tensor(impl[:, t, cols], b_val[:, t, cols], 0.5, a_val[:, t, cols], ALU.add, ALU.subtract)
-            for t in (3, 0, 1, 2):
-                nc.vector.scalar_tensor_tensor(best[:, t, cols], impl[:, t, cols], 0.5, conj[:, t, cols], ALU.min, ALU.max)
-            for t in (3, 0, 1, 2):
-                nc.vector.tensor_scalar(z_rows[:, t, cols], best[:, t, cols], 0.0, gain[:, t : t + 1], ALU.max, ALU.mult)
-            nc.vector.tensor_copy(
-                z_bf[:, cols, :].rearrange("p (c i) t -> p c t i", i=4),
-                z_rows[:, :, cols].rearrange("p t (c i) -> p c t i", i=4),
-            )
-            nc.vector.quantize_mx(z_code[:, cols].bitcast(FP8X4), z_scale[:, cols], z_bf[:, cols, :].rearrange("p j t -> p (j t)"))
-
-        def project(j0, width, bank, last):
-            cols = slice(j0, j0 + width)
+        def project(cols, bank, last):
+            width = cols.stop - cols.start
             for half in range(2):
                 acc = psum.tile([P, 2, width], F32, tag=f"bank{bank + half}")
                 for u in range(2):
                     m = slice((2 * half + u) * P, (2 * half + u + 1) * P)
                     nc.tensor.matmul_mx(acc[:, u, :], w2_code[:, m].bitcast(FP8X4), w2_scale[:, m],
                                         z_code[:, cols].bitcast(FP8X4), z_scale[:, cols], start=True, stop=True)
-                res = keep.tile([P, 2, width], F32, name=f"res{j0}_{half}")
+                res = keep.tile([P, 2, width], F32, name=f"res{cols.start}_{half}")
                 if last and half == 1:
                     nc.vector.tensor_copy(res[:], acc[:])
-                    nc.sync.dma_start(out_view[:, 2 * half : 2 * half + 2, cols], res[:])
                 else:
                     nc.scalar.copy(res[:], acc[:])
-                    nc.sync.dma_start(out_view[:, 2 * half : 2 * half + 2, cols], res[:])
+                queue = nc.scalar if last and half == 0 else nc.sync
+                queue.dma_start(out_view[:, 2 * half : 2 * half + 2, cols], res[:])
 
-        starts = [sum(CHUNKS[:i]) for i in range(len(CHUNKS))]
-        for i, (j0, width) in enumerate(zip(starts, CHUNKS)):
-            look_up(j0, width)
-            logic(j0, width)
-        for i, (j0, width) in enumerate(zip(starts, CHUNKS)):
-            project(j0, width, (6 + 2 * i) % 8, i == len(CHUNKS) - 1)
+        chunks = [slice(sum(CHUNKS[:i]), sum(CHUNKS[: i + 1])) for i in range(len(CHUNKS))]
+        pair, single = slice(1, 3), slice(3, 4)
+        for piece in pieces:
+            inside = [cols for cols in chunks if piece.start <= cols.start < piece.stop]
+            look_up(1, piece)
+            look_up(2, piece)
+            for cols in inside:
+                look_up(3, cols)
+        for piece in pieces:
+            inside = [cols for cols in chunks if piece.start <= cols.start < piece.stop]
+            conjunction(pair, piece)
+            implication(pair, piece)
+            conjunction(single, inside[0])
+            larger(pair, piece)
+            implication(single, inside[0])
+            scale_rows(pair, piece)
+            for cols, following in zip(inside, inside[1:] + [None]):
+                larger(single, cols)
+                if following:
+                    conjunction(single, following)
+                scale_rows(single, cols)
+                if following:
+                    implication(single, following)
+                interleave(cols)
+                quantize_z(cols)
+        for i, cols in enumerate(chunks):
+            project(cols, (6 + 2 * i) % 8, i == len(chunks) - 1)

@@ -40,21 +40,23 @@ def tile_picked_lukaslog_none_p_kernel(tc, x_words, x_scales, w1, gn, w2, offs, 
         nc.sync.dma_start(offs_sb[:], offs)
         w1_raw = keep.tile([P, PACK, H], F32)
         nc.sync.dma_start(w1_raw[:], w1.rearrange("(p j) h -> p j h", j=PACK))
-        for q in range(4):
+        for r in range(4):
             nc.sync.dma_start(
-                x_scale_table[32 * q : 32 * q + 4, :].bitcast(I32),
-                x_scales[0, 4 * q : 4 * q + 4, :].bitcast(I32),
+                x_scale_table[r:P:32, :].bitcast(I32),
+                x_scales[0, r:16:4, :].bitcast(I32),
             )
         x_word_table = keep.tile([P, T], I32, align_bytes=64)
         nc.sync.dma_start(x_word_table[:], x_words[0].rearrange("p n j -> p (n j)").bitcast(I32))
+        w2_rows = w2.rearrange("(p j) n -> p j n", j=PACK)
+        w2_raw = [keep.tile([P, PACK, PIECE], F32, name=f"w2_raw{h}") for h in range(2)]
+        nc.sync.dma_start(w2_raw[0][:], w2_rows[:, :, :PIECE])
         c1_sb = keep.tile([P, S // 16], U16)
         nc.sync.dma_start(c1_sb[:], c1)
         c3_sb = keep.tile([P, S // 16], U16)
         nc.sync.dma_start(c3_sb[:], c3)
         c2_sb = keep.tile([P, S // 16], U16)
         nc.sync.dma_start(c2_sb[:], c2)
-        w2_raw = keep.tile([P, PACK, N], F32)
-        nc.sync.dma_start(w2_raw[:], w2.rearrange("(p j) n -> p j n", j=PACK))
+        nc.sync.dma_start(w2_raw[1][:], w2_rows[:, :, PIECE:])
         gain = keep.tile([P, PACK], F32)
         nc.sync.dma_start(gain[:], gn.rearrange("(p t) o -> p (t o)", t=PACK))
 
@@ -73,8 +75,11 @@ def tile_picked_lukaslog_none_p_kernel(tc, x_words, x_scales, w1, gn, w2, offs, 
             nc.vector.quantize_mx(w1_code[:, cols].bitcast(FP8X4), w1_scale[:, cols], w1_bf[:, t0 : t0 + 2].rearrange("p t m j -> p (t m j)"))
 
         x_code = keep.tile([P, S], U32, align_bytes=64)
-        truth = keep.tile([P, S], F32)
-        logit = {t: keep.tile([P, S], F32, name=f"logit{t}") for t in (1, 2, 3)}
+        truth = keep.tile([P, 2 * S], F32)
+        truth_less = keep.tile([P, 2 * S], F32)
+        logit = {t: keep.tile([P, 2 * S if t == 1 else S], F32, name=f"logit{t}") for t in (1, 2, 3)}
+        for window in (truth, truth_less, logit[1]):
+            nc.vector.memset(window[:, S:], 0.0)
 
         def first_product(t, j0, width, bank):
             cols = slice(t * P, (t + 1) * P)
@@ -87,10 +92,10 @@ def tile_picked_lukaslog_none_p_kernel(tc, x_words, x_scales, w1, gn, w2, offs, 
         for h in range(2):
             cols = slice(h * PIECE, (h + 1) * PIECE)
             nc.vector.tensor_copy(x_code[:, cols], x_word_table[:].bitcast(U32).indirect(offs_sb[:, h * PIECE // 16 : (h + 1) * PIECE // 16]))
-            hid0 = first_product(0, h * PIECE, PIECE, h)
             hid1 = first_product(1, h * PIECE, PIECE, 2 + h)
-            nc.scalar.activation(truth[:, cols], hid0[:], ACT.Sigmoid, scale=2.0)
+            hid0 = first_product(0, h * PIECE, PIECE, h)
             nc.scalar.copy(logit[1][:, cols], hid1[:])
+            nc.scalar.activation(truth[:, cols], hid0[:], ACT.Sigmoid, scale=2.0)
         quantize_w1(2)
         hid = {t: first_product(t, 0, S, 2 + t) for t in (2, 3)}
 
@@ -100,11 +105,10 @@ def tile_picked_lukaslog_none_p_kernel(tc, x_words, x_scales, w1, gn, w2, offs, 
         b_val = keep.tile([P, PACK, S], F32)
         c_val = keep.tile([P, PACK, S], F32)
         best = keep.tile([P, PACK, S], F32)
-        z_rows = keep.tile([P, PACK, S], BF16)
+        z_rows = keep.tile([P, 3, S], BF16)
         z_bf = keep.tile([P, S, PACK], BF16, align_bytes=64)
         z_code = keep.tile([P, S], U32, align_bytes=64)
         z_scale = keep.tile([P, S], U8, align_bytes=64)
-        truth_less = keep.tile([P, S], F32)
         out_view = out.rearrange("(u p) j -> p u j", p=P)
 
         def entries(lst, cols):
@@ -125,37 +129,34 @@ def tile_picked_lukaslog_none_p_kernel(tc, x_words, x_scales, w1, gn, w2, offs, 
         def larger(ts, cols):
             nc.vector.scalar_tensor_tensor(best[:, ts, cols], impl[:, ts, cols], 0.5, conj[:, ts, cols], ALU.min, ALU.max)
 
-        def scale_rows(ts, cols):
-            for t in range(ts.start, ts.stop):
-                nc.vector.tensor_scalar(z_rows[:, t, cols], best[:, t, cols], 0.0, gain[:, t : t + 1], ALU.max, ALU.mult)
+        def scale_rows(t, cols):
+            dst = z_bf[:, cols, t] if t == 3 else z_rows[:, t, cols]
+            nc.vector.tensor_scalar(dst, best[:, t, cols], 0.0, gain[:, t : t + 1], ALU.max, ALU.mult)
 
         def interleave(cols):
             nc.vector.tensor_copy(
-                z_bf[:, cols, :].rearrange("p (c i) t -> p c t i", i=4),
+                z_bf[:, cols, :3].rearrange("p (c i) t -> p c t i", i=4),
                 z_rows[:, :, cols].rearrange("p t (c i) -> p c t i", i=4),
             )
 
         def quantize_z(cols):
             nc.vector.quantize_mx(z_code[:, cols].bitcast(FP8X4), z_scale[:, cols], z_bf[:, cols, :].rearrange("p j t -> p (j t)"))
 
-        nc.scalar.activation(truth_less[:], truth[:], ACT.Copy, bias=-0.5)
-        pieces = [slice(j0, j0 + PIECE) for j0 in range(0, S, PIECE)]
-        for cols in pieces:
-            nc.vector.tensor_scalar(a_val[:, 0, cols], truth[:].indirect(entries(c1_sb, cols)), 1.0, -1.0, ALU.mult, ALU.add)
-        for cols in pieces:
-            nc.vector.tensor_tensor(conj[:, 0, cols], truth[:].indirect(entries(c3_sb, cols)), a_val[:, 0, cols], ALU.add)
-            nc.vector.tensor_tensor(impl[:, 0, cols], truth_less[:].indirect(entries(c2_sb, cols)), a_val[:, 0, cols], ALU.subtract)
-
         w2_bf = keep.tile([P, N, PACK], BF16, align_bytes=64)
-        nc.vector.tensor_copy(
-            w2_bf[:].rearrange("p (c i) j -> p c j i", i=4),
-            w2_raw[:].rearrange("p j (c i) -> p c j i", i=4),
-        )
-        larger(slice(0, 1), slice(0, S))
+        for h in range(2):
+            nc.vector.tensor_copy(
+                w2_bf[:, h * PIECE : (h + 1) * PIECE].rearrange("p (c i) j -> p c j i", i=4),
+                w2_raw[h][:].rearrange("p j (c i) -> p c j i", i=4),
+            )
         w2_code = keep.tile([P, N], U32, align_bytes=64)
         w2_scale = keep.tile([P, N], U8, align_bytes=64)
         nc.vector.quantize_mx(w2_code[:].bitcast(FP8X4), w2_scale[:], w2_bf[:].rearrange("p n j -> p (n j)"))
-        scale_rows(slice(0, 1), slice(0, S))
+        nc.vector.tensor_scalar(a_val[:, 0], truth[:].indirect(c1_sb[:]), 1.0, -1.0, ALU.mult, ALU.add)
+        nc.vector.tensor_scalar(truth_less[:, :S], truth[:, :S], -0.5, None, ALU.add)
+        nc.vector.tensor_tensor(conj[:, 0], truth[:].indirect(c3_sb[:]), a_val[:, 0], ALU.add)
+        nc.vector.tensor_tensor(impl[:, 0], truth_less[:].indirect(c2_sb[:]), a_val[:, 0], ALU.subtract)
+        larger(slice(0, 1), slice(0, S))
+        scale_rows(0, slice(0, S))
 
         def project(cols, bank, last):
             width = cols.stop - cols.start
@@ -174,29 +175,21 @@ def tile_picked_lukaslog_none_p_kernel(tc, x_words, x_scales, w1, gn, w2, offs, 
                 queue.dma_start(out_view[:, 2 * half : 2 * half + 2, cols], res[:])
 
         chunks = [slice(sum(CHUNKS[:i]), sum(CHUNKS[: i + 1])) for i in range(len(CHUNKS))]
-        pair, single = slice(1, 3), slice(3, 4)
-        for piece in pieces:
-            inside = [cols for cols in chunks if piece.start <= cols.start < piece.stop]
-            look_up(1, piece)
-            look_up(2, piece)
-            for cols in inside:
-                look_up(3, cols)
-        for piece in pieces:
-            inside = [cols for cols in chunks if piece.start <= cols.start < piece.stop]
-            conjunction(pair, piece)
-            implication(pair, piece)
-            conjunction(single, inside[0])
-            larger(pair, piece)
-            implication(single, inside[0])
-            scale_rows(pair, piece)
-            for cols, following in zip(inside, inside[1:] + [None]):
-                larger(single, cols)
-                if following:
-                    conjunction(single, following)
-                scale_rows(single, cols)
-                if following:
-                    implication(single, following)
+        units = [(1, slice(0, S))]
+        for j0 in range(0, S, PIECE):
+            units.append((2, slice(j0, j0 + PIECE)))
+            units += [(3, cols) for cols in chunks if j0 <= cols.start < j0 + PIECE]
+        for t, cols in units:
+            look_up(t, cols)
+        for t, cols in units:
+            ts = slice(t, t + 1)
+            conjunction(ts, cols)
+            implication(ts, cols)
+            larger(ts, cols)
+            scale_rows(t, cols)
+            if t == 2:
                 interleave(cols)
+            if t == 3:
                 quantize_z(cols)
         for i, cols in enumerate(chunks):
             project(cols, (6 + 2 * i) % 8, i == len(chunks) - 1)

@@ -17,9 +17,11 @@ ACT = mybir.ActivationFunctionType
 
 P = 128
 PACK = 4
+LIST_ROWS = 16
+HALF = 256
+LAST_TILE = PACK - 1
 CHUNKS = (256, 128, 128)
-PIECE = 256
-W1_SCALAR_M = 72
+PSUM_BANKS = 8
 
 
 def tile_picked_lukaslog_none_p_kernel(tc, x_words, x_scales, w1, gn, w2, offs, c1, c2, c3, out):
@@ -31,48 +33,54 @@ def tile_picked_lukaslog_none_p_kernel(tc, x_words, x_scales, w1, gn, w2, offs, 
         x_scale_table = keep.tile([P, T], U8, align_bytes=64, tag="scale_table_then_w1_code")
         nc.vector.memset(x_scale_table[:].bitcast(I32), 0)
 
-        warm_in = keep.tile([P, 1], F32)
-        nc.gpsimd.memset(warm_in[:], 0.0)
-        warm_out = keep.tile([P, 1], F32)
-        nc.scalar.activation(warm_out[:], warm_in[:], ACT.Sigmoid, scale=2.0)
-
-        offs_sb = keep.tile([P, S // 16], U16)
+        offs_sb = keep.tile([P, S // LIST_ROWS], U16)
         nc.sync.dma_start(offs_sb[:], offs)
         w1_raw = keep.tile([P, PACK, H], F32)
-        nc.sync.dma_start(w1_raw[:], w1.rearrange("(p j) h -> p j h", j=PACK))
+        nc.sync.dma_start(w1_raw[:], w1.rearrange("(p j) i -> p j i", j=PACK))
         for r in range(4):
             nc.sync.dma_start(
                 x_scale_table[r:P:32, :].bitcast(I32),
                 x_scales[0, r:16:4, :].bitcast(I32),
             )
-        x_word_table = keep.tile([P, T], I32, align_bytes=64)
+        x_word_table = keep.tile([P, T], I32, align_bytes=64, tag="word_table_then_w1_bf")
         nc.sync.dma_start(x_word_table[:], x_words[0].rearrange("p n j -> p (n j)").bitcast(I32))
         w2_rows = w2.rearrange("(p j) n -> p j n", j=PACK)
-        w2_raw = [keep.tile([P, PACK, PIECE], F32, name=f"w2_raw{h}") for h in range(2)]
-        nc.sync.dma_start(w2_raw[0][:], w2_rows[:, :, :PIECE])
-        c1_sb = keep.tile([P, S // 16], U16)
+        w2_raw = [keep.tile([P, PACK, HALF], F32, name=f"w2_raw{h}") for h in range(2)]
+        nc.sync.dma_start(w2_raw[0][:], w2_rows[:, :, :HALF])
+        c1_sb = keep.tile([P, S // LIST_ROWS], U16)
         nc.sync.dma_start(c1_sb[:], c1)
-        c3_sb = keep.tile([P, S // 16], U16)
+        c3_sb = keep.tile([P, S // LIST_ROWS], U16)
         nc.sync.dma_start(c3_sb[:], c3)
-        c2_sb = keep.tile([P, S // 16], U16)
+        c2_sb = keep.tile([P, S // LIST_ROWS], U16)
         nc.sync.dma_start(c2_sb[:], c2)
-        nc.sync.dma_start(w2_raw[1][:], w2_rows[:, :, PIECE:])
+        nc.sync.dma_start(w2_raw[1][:], w2_rows[:, :, HALF:])
         gain = keep.tile([P, PACK], F32)
         nc.sync.dma_start(gain[:], gn.rearrange("(p t) o -> p (t o)", t=PACK))
 
-        w1_bf = keep.tile([P, PACK, P, PACK], BF16, align_bytes=64)
-        w1_dst = w1_bf[:].rearrange("p t m j -> p m j t")
-        w1_src = w1_raw[:].rearrange("p j (m t) -> p m j t", t=PACK)
-        nc.scalar.copy(w1_dst[:, :W1_SCALAR_M], w1_src[:, :W1_SCALAR_M])
-        nc.vector.tensor_copy(w1_dst[:, W1_SCALAR_M:], w1_src[:, W1_SCALAR_M:])
+        def entries(list_sb, cols):
+            return list_sb[:, cols.start // LIST_ROWS : cols.stop // LIST_ROWS]
+
+        def cast_w1(t0, tag):
+            w1_bf = keep.tile([P, 2, P, PACK], BF16, align_bytes=64, tag=tag)
+            nc.vector.tensor_copy(
+                w1_bf[:].rearrange("p t m j -> p m j t"),
+                w1_raw[:].rearrange("p j (m t) -> p m j t", t=PACK)[:, :, :, t0 : t0 + 2],
+            )
+            return w1_bf
+
+        w1_bf_low = cast_w1(0, "w1_bf_low")
         x_scale = keep.tile([P, S], U8, align_bytes=64)
         nc.vector.tensor_copy(x_scale[:], x_scale_table[:].indirect(offs_sb[:]))
         w1_code = keep.tile([P, H], U32, align_bytes=64, tag="scale_table_then_w1_code")
         w1_scale = keep.tile([P, H], U8, align_bytes=64)
 
-        def quantize_w1(t0):
-            cols = slice(t0 * P, (t0 + 2) * P)
-            nc.vector.quantize_mx(w1_code[:, cols].bitcast(FP8X4), w1_scale[:, cols], w1_bf[:, t0 : t0 + 2].rearrange("p t m j -> p (t m j)"))
+        def quantize_w1(t0, w1_bf):
+            code_cols = slice(t0 * P, (t0 + 2) * P)
+            nc.vector.quantize_mx(
+                w1_code[:, code_cols].bitcast(FP8X4),
+                w1_scale[:, code_cols],
+                w1_bf[:].rearrange("p t m j -> p (t m j)"),
+            )
 
         x_code = keep.tile([P, S], U32, align_bytes=64)
         truth = keep.tile([P, 2 * S], F32)
@@ -81,23 +89,33 @@ def tile_picked_lukaslog_none_p_kernel(tc, x_words, x_scales, w1, gn, w2, offs, 
         for window in (truth, truth_less, logit[1]):
             nc.vector.memset(window[:, S:], 0.0)
 
-        def first_product(t, j0, width, bank):
-            cols = slice(t * P, (t + 1) * P)
-            hid = psum.tile([P, width], F32, tag=f"bank{bank}")
-            nc.tensor.matmul_mx(hid[:], w1_code[:, cols].bitcast(FP8X4), w1_scale[:, cols],
-                                x_code[:, j0 : j0 + width].bitcast(FP8X4), x_scale[:, j0 : j0 + width], start=True, stop=True)
+        def first_product(t, cols, bank):
+            code_cols = slice(t * P, (t + 1) * P)
+            hid = psum.tile([P, cols.stop - cols.start], F32, tag=f"bank{bank}")
+            nc.tensor.matmul_mx(
+                hid[:],
+                w1_code[:, code_cols].bitcast(FP8X4),
+                w1_scale[:, code_cols],
+                x_code[:, cols].bitcast(FP8X4),
+                x_scale[:, cols],
+                start=True,
+                stop=True,
+            )
             return hid
 
-        quantize_w1(0)
-        for h in range(2):
-            cols = slice(h * PIECE, (h + 1) * PIECE)
-            nc.vector.tensor_copy(x_code[:, cols], x_word_table[:].bitcast(U32).indirect(offs_sb[:, h * PIECE // 16 : (h + 1) * PIECE // 16]))
-            hid1 = first_product(1, h * PIECE, PIECE, 2 + h)
-            hid0 = first_product(0, h * PIECE, PIECE, h)
-            nc.scalar.copy(logit[1][:, cols], hid1[:])
-            nc.scalar.activation(truth[:, cols], hid0[:], ACT.Sigmoid, scale=2.0)
-        quantize_w1(2)
-        hid = {t: first_product(t, 0, S, 2 + t) for t in (2, 3)}
+        halves = [slice(h * HALF, (h + 1) * HALF) for h in range(2)]
+        quantize_w1(0, w1_bf_low)
+        for h, cols in enumerate(halves):
+            nc.vector.tensor_copy(x_code[:, cols], x_word_table[:].bitcast(U32).indirect(entries(offs_sb, cols)))
+            for t in (h, 1 - h):
+                hid = first_product(t, cols, 2 * t + h)
+                if t == 0:
+                    nc.scalar.activation(truth[:, cols], hid[:], ACT.Sigmoid, scale=2.0)
+                else:
+                    nc.scalar.copy(logit[1][:, cols], hid[:])
+        quantize_w1(2, cast_w1(2, "word_table_then_w1_bf"))
+        whole = slice(0, S)
+        hid_whole = {t: first_product(t, whole, 2 + t) for t in (2, 3)}
 
         conj = keep.tile([P, PACK, S], F32)
         impl = keep.tile([P, PACK, S], F32)
@@ -105,91 +123,99 @@ def tile_picked_lukaslog_none_p_kernel(tc, x_words, x_scales, w1, gn, w2, offs, 
         b_val = keep.tile([P, PACK, S], F32)
         c_val = keep.tile([P, PACK, S], F32)
         best = keep.tile([P, PACK, S], F32)
-        z_rows = keep.tile([P, 3, S], BF16)
+        z_rows = keep.tile([P, LAST_TILE, S], BF16)
         z_bf = keep.tile([P, S, PACK], BF16, align_bytes=64)
         z_code = keep.tile([P, S], U32, align_bytes=64)
         z_scale = keep.tile([P, S], U8, align_bytes=64)
-        out_view = out.rearrange("(u p) j -> p u j", p=P)
-
-        def entries(lst, cols):
-            return lst[:, cols.start // 16 : cols.stop // 16]
 
         def look_up(t, cols):
-            if cols.start == 0 and t > 1:
-                nc.scalar.copy(logit[t][:], hid[t][:])
-            for val, lst in ((a_val, c1_sb), (c_val, c3_sb), (b_val, c2_sb)):
-                nc.scalar.activation(val[:, t, cols], logit[t][:].indirect(entries(lst, cols)), ACT.Sigmoid, scale=2.0)
+            if cols.start == 0 and t in hid_whole:
+                nc.scalar.copy(logit[t][:], hid_whole[t][:])
+            for val, list_sb in ((a_val, c1_sb), (c_val, c3_sb), (b_val, c2_sb)):
+                nc.scalar.activation(val[:, t, cols], logit[t][:].indirect(entries(list_sb, cols)), ACT.Sigmoid, scale=2.0)
 
-        def conjunction(ts, cols):
-            nc.vector.scalar_tensor_tensor(conj[:, ts, cols], a_val[:, ts, cols], -1.0, c_val[:, ts, cols], ALU.add, ALU.add)
+        def conjunction(t, cols):
+            nc.vector.scalar_tensor_tensor(conj[:, t, cols], a_val[:, t, cols], -1.0, c_val[:, t, cols], ALU.add, ALU.add)
 
-        def implication(ts, cols):
-            nc.vector.scalar_tensor_tensor(impl[:, ts, cols], b_val[:, ts, cols], 0.5, a_val[:, ts, cols], ALU.add, ALU.subtract)
+        def implication(t, cols):
+            nc.vector.scalar_tensor_tensor(impl[:, t, cols], b_val[:, t, cols], 0.5, a_val[:, t, cols], ALU.add, ALU.subtract)
 
-        def larger(ts, cols):
-            nc.vector.scalar_tensor_tensor(best[:, ts, cols], impl[:, ts, cols], 0.5, conj[:, ts, cols], ALU.min, ALU.max)
+        def larger(t, cols):
+            nc.vector.scalar_tensor_tensor(best[:, t, cols], impl[:, t, cols], 0.5, conj[:, t, cols], ALU.min, ALU.max)
 
         def scale_rows(t, cols):
-            dst = z_bf[:, cols, t] if t == 3 else z_rows[:, t, cols]
+            dst = z_bf[:, cols, t] if t == LAST_TILE else z_rows[:, t, cols]
             nc.vector.tensor_scalar(dst, best[:, t, cols], 0.0, gain[:, t : t + 1], ALU.max, ALU.mult)
 
         def interleave(cols):
             nc.vector.tensor_copy(
-                z_bf[:, cols, :3].rearrange("p (c i) t -> p c t i", i=4),
-                z_rows[:, :, cols].rearrange("p t (c i) -> p c t i", i=4),
+                z_bf[:, cols, :LAST_TILE].rearrange("p (c s) t -> p c t s", s=4),
+                z_rows[:, :, cols].rearrange("p t (c s) -> p c t s", s=4),
             )
 
         def quantize_z(cols):
-            nc.vector.quantize_mx(z_code[:, cols].bitcast(FP8X4), z_scale[:, cols], z_bf[:, cols, :].rearrange("p j t -> p (j t)"))
+            nc.vector.quantize_mx(
+                z_code[:, cols].bitcast(FP8X4), z_scale[:, cols], z_bf[:, cols, :].rearrange("p n t -> p (n t)")
+            )
 
         w2_bf = keep.tile([P, N, PACK], BF16, align_bytes=64)
-        for h in range(2):
+        for h, w2_cols in enumerate(halves):
             nc.vector.tensor_copy(
-                w2_bf[:, h * PIECE : (h + 1) * PIECE].rearrange("p (c i) j -> p c j i", i=4),
-                w2_raw[h][:].rearrange("p j (c i) -> p c j i", i=4),
+                w2_bf[:, w2_cols].rearrange("p (c s) j -> p c j s", s=4),
+                w2_raw[h][:].rearrange("p j (c s) -> p c j s", s=4),
             )
         w2_code = keep.tile([P, N], U32, align_bytes=64)
         w2_scale = keep.tile([P, N], U8, align_bytes=64)
         nc.vector.quantize_mx(w2_code[:].bitcast(FP8X4), w2_scale[:], w2_bf[:].rearrange("p n j -> p (n j)"))
+
         nc.vector.tensor_scalar(a_val[:, 0], truth[:].indirect(c1_sb[:]), 1.0, -1.0, ALU.mult, ALU.add)
         nc.vector.tensor_scalar(truth_less[:, :S], truth[:, :S], -0.5, None, ALU.add)
         nc.vector.tensor_tensor(conj[:, 0], truth[:].indirect(c3_sb[:]), a_val[:, 0], ALU.add)
         nc.vector.tensor_tensor(impl[:, 0], truth_less[:].indirect(c2_sb[:]), a_val[:, 0], ALU.subtract)
-        larger(slice(0, 1), slice(0, S))
-        scale_rows(0, slice(0, S))
+        larger(0, whole)
+        scale_rows(0, whole)
 
-        def project(cols, bank, last):
+        chunks = [slice(sum(CHUNKS[:chunk]), sum(CHUNKS[: chunk + 1])) for chunk in range(len(CHUNKS))]
+        steps = [(1, whole)]
+        for half in halves:
+            steps.append((2, half))
+            steps += [(LAST_TILE, cols) for cols in chunks if half.start <= cols.start < half.stop]
+        for t, cols in steps:
+            look_up(t, cols)
+        for t, cols in steps:
+            conjunction(t, cols)
+            implication(t, cols)
+            larger(t, cols)
+            scale_rows(t, cols)
+            if t == LAST_TILE - 1:
+                interleave(cols)
+            if t == LAST_TILE:
+                quantize_z(cols)
+
+        out_view = out.rearrange("(u p) n -> p u n", p=P)
+
+        def second_product(cols, first_bank, last):
             width = cols.stop - cols.start
-            for half in range(2):
-                acc = psum.tile([P, 2, width], F32, tag=f"bank{bank + half}")
+            for pair in range(2):
+                acc = psum.tile([P, 2, width], F32, tag=f"bank{first_bank + pair}")
                 for u in range(2):
-                    m = slice((2 * half + u) * P, (2 * half + u + 1) * P)
-                    nc.tensor.matmul_mx(acc[:, u, :], w2_code[:, m].bitcast(FP8X4), w2_scale[:, m],
-                                        z_code[:, cols].bitcast(FP8X4), z_scale[:, cols], start=True, stop=True)
-                res = keep.tile([P, 2, width], F32, name=f"res{cols.start}_{half}")
-                if last and half == 1:
+                    rows = slice((2 * pair + u) * P, (2 * pair + u + 1) * P)
+                    nc.tensor.matmul_mx(
+                        acc[:, u, :],
+                        w2_code[:, rows].bitcast(FP8X4),
+                        w2_scale[:, rows],
+                        z_code[:, cols].bitcast(FP8X4),
+                        z_scale[:, cols],
+                        start=True,
+                        stop=True,
+                    )
+                res = keep.tile([P, 2, width], F32, name=f"res{cols.start}_{pair}")
+                if last and pair == 1:
                     nc.vector.tensor_copy(res[:], acc[:])
                 else:
                     nc.scalar.copy(res[:], acc[:])
-                queue = nc.scalar if last and half == 0 else nc.sync
-                queue.dma_start(out_view[:, 2 * half : 2 * half + 2, cols], res[:])
+                queue = nc.scalar if last and pair == 0 else nc.sync
+                queue.dma_start(out_view[:, 2 * pair : 2 * pair + 2, cols], res[:])
 
-        chunks = [slice(sum(CHUNKS[:i]), sum(CHUNKS[: i + 1])) for i in range(len(CHUNKS))]
-        units = [(1, slice(0, S))]
-        for j0 in range(0, S, PIECE):
-            units.append((2, slice(j0, j0 + PIECE)))
-            units += [(3, cols) for cols in chunks if j0 <= cols.start < j0 + PIECE]
-        for t, cols in units:
-            look_up(t, cols)
-        for t, cols in units:
-            ts = slice(t, t + 1)
-            conjunction(ts, cols)
-            implication(ts, cols)
-            larger(ts, cols)
-            scale_rows(t, cols)
-            if t == 2:
-                interleave(cols)
-            if t == 3:
-                quantize_z(cols)
-        for i, cols in enumerate(chunks):
-            project(cols, (6 + 2 * i) % 8, i == len(chunks) - 1)
+        for chunk, cols in enumerate(chunks):
+            second_product(cols, (6 + 2 * chunk) % PSUM_BANKS, chunk == len(chunks) - 1)

from contextlib import ExitStack

import concourse.mybir as mybir

K, T, S, N, H = 512, 2048, 512, 512, 512
FLOPS = 2 * K * H * S + 2 * H * N * S

F32 = mybir.dt.float32
BF16 = mybir.dt.bfloat16
I32 = mybir.dt.int32
U32 = mybir.dt.uint32
U16 = mybir.dt.uint16
U8 = mybir.dt.uint8
FP8X4 = mybir.dt.float8_e4m3fn_x4
ALU = mybir.AluOpType
ACT = mybir.ActivationFunctionType

P = 128
PACK = 4
LIST_ROWS = 16
HALF = 256
LAST_TILE = PACK - 1
CHUNKS = (256, 128, 128)
PSUM_BANKS = 8


def tile_picked_lukaslog_none_p_kernel(tc, x_words, x_scales, w1, gn, w2, offs, c1, c2, c3, out):
    nc = tc.nc
    with ExitStack() as ctx:
        keep = ctx.enter_context(tc.tile_pool(name="keep", bufs=1))
        psum = ctx.enter_context(tc.psum_pool(name="psum", bufs=1))

        x_scale_table = keep.tile([P, T], U8, align_bytes=64, tag="scale_table_then_w1_code")
        nc.vector.memset(x_scale_table[:].bitcast(I32), 0)

        offs_sb = keep.tile([P, S // LIST_ROWS], U16)
        nc.sync.dma_start(offs_sb[:], offs)
        w1_raw = keep.tile([P, PACK, H], F32)
        nc.sync.dma_start(w1_raw[:], w1.rearrange("(p j) i -> p j i", j=PACK))
        for r in range(4):
            nc.sync.dma_start(
                x_scale_table[r:P:32, :].bitcast(I32),
                x_scales[0, r:16:4, :].bitcast(I32),
            )
        x_word_table = keep.tile([P, T], I32, align_bytes=64, tag="word_table_then_w1_bf")
        nc.sync.dma_start(x_word_table[:], x_words[0].rearrange("p n j -> p (n j)").bitcast(I32))
        w2_rows = w2.rearrange("(p j) n -> p j n", j=PACK)
        w2_raw = [keep.tile([P, PACK, HALF], F32, name=f"w2_raw{h}") for h in range(2)]
        nc.sync.dma_start(w2_raw[0][:], w2_rows[:, :, :HALF])
        c1_sb = keep.tile([P, S // LIST_ROWS], U16)
        nc.sync.dma_start(c1_sb[:], c1)
        c3_sb = keep.tile([P, S // LIST_ROWS], U16)
        nc.sync.dma_start(c3_sb[:], c3)
        c2_sb = keep.tile([P, S // LIST_ROWS], U16)
        nc.sync.dma_start(c2_sb[:], c2)
        nc.sync.dma_start(w2_raw[1][:], w2_rows[:, :, HALF:])
        gain = keep.tile([P, PACK], F32)
        nc.sync.dma_start(gain[:], gn.rearrange("(p t) o -> p (t o)", t=PACK))

        def entries(list_sb, cols):
            return list_sb[:, cols.start // LIST_ROWS : cols.stop // LIST_ROWS]

        def cast_w1(t0, tag):
            w1_bf = keep.tile([P, 2, P, PACK], BF16, align_bytes=64, tag=tag)
            nc.vector.tensor_copy(
                w1_bf[:].rearrange("p t m j -> p m j t"),
                w1_raw[:].rearrange("p j (m t) -> p m j t", t=PACK)[:, :, :, t0 : t0 + 2],
            )
            return w1_bf

        w1_bf_low = cast_w1(0, "w1_bf_low")
        x_scale = keep.tile([P, S], U8, align_bytes=64)
        nc.vector.tensor_copy(x_scale[:], x_scale_table[:].indirect(offs_sb[:]))
        w1_code = keep.tile([P, H], U32, align_bytes=64, tag="scale_table_then_w1_code")
        w1_scale = keep.tile([P, H], U8, align_bytes=64)

        def quantize_w1(t0, w1_bf):
            code_cols = slice(t0 * P, (t0 + 2) * P)
            nc.vector.quantize_mx(
                w1_code[:, code_cols].bitcast(FP8X4),
                w1_scale[:, code_cols],
                w1_bf[:].rearrange("p t m j -> p (t m j)"),
            )

        x_code = keep.tile([P, S], U32, align_bytes=64)
        truth = keep.tile([P, 2 * S], F32)
        truth_less = keep.tile([P, 2 * S], F32)
        logit = {t: keep.tile([P, 2 * S if t == 1 else S], F32, name=f"logit{t}") for t in (1, 2, 3)}
        for window in (truth, truth_less, logit[1]):
            nc.vector.memset(window[:, S:], 0.0)

        def first_product(t, cols, bank):
            code_cols = slice(t * P, (t + 1) * P)
            hid = psum.tile([P, cols.stop - cols.start], F32, tag=f"bank{bank}")
            nc.tensor.matmul_mx(
                hid[:],
                w1_code[:, code_cols].bitcast(FP8X4),
                w1_scale[:, code_cols],
                x_code[:, cols].bitcast(FP8X4),
                x_scale[:, cols],
                start=True,
                stop=True,
            )
            return hid

        halves = [slice(h * HALF, (h + 1) * HALF) for h in range(2)]
        quantize_w1(0, w1_bf_low)
        for h, cols in enumerate(halves):
            nc.vector.tensor_copy(x_code[:, cols], x_word_table[:].bitcast(U32).indirect(entries(offs_sb, cols)))
            for t in (h, 1 - h):
                hid = first_product(t, cols, 2 * t + h)
                if t == 0:
                    nc.scalar.activation(truth[:, cols], hid[:], ACT.Sigmoid, scale=2.0)
                else:
                    nc.scalar.copy(logit[1][:, cols], hid[:])
        quantize_w1(2, cast_w1(2, "word_table_then_w1_bf"))
        whole = slice(0, S)
        hid_whole = {t: first_product(t, whole, 2 + t) for t in (2, 3)}

        conj = keep.tile([P, PACK, S], F32)
        impl = keep.tile([P, PACK, S], F32)
        a_val = keep.tile([P, PACK, S], F32)
        b_val = keep.tile([P, PACK, S], F32)
        c_val = keep.tile([P, PACK, S], F32)
        best = keep.tile([P, PACK, S], F32)
        z_rows = keep.tile([P, LAST_TILE, S], BF16)
        z_bf = keep.tile([P, S, PACK], BF16, align_bytes=64)
        z_code = keep.tile([P, S], U32, align_bytes=64)
        z_scale = keep.tile([P, S], U8, align_bytes=64)

        def look_up(t, cols):
            if cols.start == 0 and t in hid_whole:
                nc.scalar.copy(logit[t][:], hid_whole[t][:])
            for val, list_sb in ((a_val, c1_sb), (c_val, c3_sb), (b_val, c2_sb)):
                nc.scalar.activation(val[:, t, cols], logit[t][:].indirect(entries(list_sb, cols)), ACT.Sigmoid, scale=2.0)

        def conjunction(t, cols):
            nc.vector.scalar_tensor_tensor(conj[:, t, cols], a_val[:, t, cols], -1.0, c_val[:, t, cols], ALU.add, ALU.add)

        def implication(t, cols):
            nc.vector.scalar_tensor_tensor(impl[:, t, cols], b_val[:, t, cols], 0.5, a_val[:, t, cols], ALU.add, ALU.subtract)

        def larger(t, cols):
            nc.vector.scalar_tensor_tensor(best[:, t, cols], impl[:, t, cols], 0.5, conj[:, t, cols], ALU.min, ALU.max)

        def scale_rows(t, cols):
            dst = z_bf[:, cols, t] if t == LAST_TILE else z_rows[:, t, cols]
            nc.vector.tensor_scalar(dst, best[:, t, cols], 0.0, gain[:, t : t + 1], ALU.max, ALU.mult)

        def interleave(cols):
            nc.vector.tensor_copy(
                z_bf[:, cols, :LAST_TILE].rearrange("p (c s) t -> p c t s", s=4),
                z_rows[:, :, cols].rearrange("p t (c s) -> p c t s", s=4),
            )

        def quantize_z(cols):
            nc.vector.quantize_mx(
                z_code[:, cols].bitcast(FP8X4), z_scale[:, cols], z_bf[:, cols, :].rearrange("p n t -> p (n t)")
            )

        w2_bf = keep.tile([P, N, PACK], BF16, align_bytes=64)
        for h, w2_cols in enumerate(halves):
            nc.vector.tensor_copy(
                w2_bf[:, w2_cols].rearrange("p (c s) j -> p c j s", s=4),
                w2_raw[h][:].rearrange("p j (c s) -> p c j s", s=4),
            )
        w2_code = keep.tile([P, N], U32, align_bytes=64)
        w2_scale = keep.tile([P, N], U8, align_bytes=64)
        nc.vector.quantize_mx(w2_code[:].bitcast(FP8X4), w2_scale[:], w2_bf[:].rearrange("p n j -> p (n j)"))

        nc.vector.tensor_scalar(a_val[:, 0], truth[:].indirect(c1_sb[:]), 1.0, -1.0, ALU.mult, ALU.add)
        nc.vector.tensor_scalar(truth_less[:, :S], truth[:, :S], -0.5, None, ALU.add)
        nc.vector.tensor_tensor(conj[:, 0], truth[:].indirect(c3_sb[:]), a_val[:, 0], ALU.add)
        nc.vector.tensor_tensor(impl[:, 0], truth_less[:].indirect(c2_sb[:]), a_val[:, 0], ALU.subtract)
        larger(0, whole)
        scale_rows(0, whole)

        chunks = [slice(sum(CHUNKS[:chunk]), sum(CHUNKS[: chunk + 1])) for chunk in range(len(CHUNKS))]
        steps = [(1, whole)]
        for half in halves:
            steps.append((2, half))
            steps += [(LAST_TILE, cols) for cols in chunks if half.start <= cols.start < half.stop]
        for t, cols in steps:
            look_up(t, cols)
        for t, cols in steps:
            conjunction(t, cols)
            implication(t, cols)
            larger(t, cols)
            scale_rows(t, cols)
            if t == LAST_TILE - 1:
                interleave(cols)
            if t == LAST_TILE:
                quantize_z(cols)

        out_view = out.rearrange("(u p) n -> p u n", p=P)

        def second_product(cols, first_bank, last):
            width = cols.stop - cols.start
            for pair in range(2):
                acc = psum.tile([P, 2, width], F32, tag=f"bank{first_bank + pair}")
                for u in range(2):
                    rows = slice((2 * pair + u) * P, (2 * pair + u + 1) * P)
                    nc.tensor.matmul_mx(
                        acc[:, u, :],
                        w2_code[:, rows].bitcast(FP8X4),
                        w2_scale[:, rows],
                        z_code[:, cols].bitcast(FP8X4),
                        z_scale[:, cols],
                        start=True,
                        stop=True,
                    )
                res = keep.tile([P, 2, width], F32, name=f"res{cols.start}_{pair}")
                if last and pair == 1:
                    nc.vector.tensor_copy(res[:], acc[:])
                else:
                    nc.scalar.copy(res[:], acc[:])
                queue = nc.scalar if last and pair == 0 else nc.sync
                queue.dma_start(out_view[:, 2 * pair : 2 * pair + 2, cols], res[:])

        for chunk, cols in enumerate(chunks):
            second_product(cols, (6 + 2 * chunk) % PSUM_BANKS, chunk == len(chunks) - 1)
